import numpy as np
import ml_dtypes


def mxq(x, axis, fmt="e4m3"):
    dtype, down = {"e4m3": (ml_dtypes.float8_e4m3fn, 7), "e5m2": (ml_dtypes.float8_e5m2, 14)}[fmt]
    v = np.moveaxis(np.asarray(x, np.float32).astype(ml_dtypes.bfloat16).astype(np.float64), axis, -1)
    blocks = v.reshape(v.shape[:-1] + (-1, 32))
    amax = np.abs(blocks).max(-1, keepdims=True)
    byte = np.maximum(np.where(amax > 0, np.frexp(amax)[1] - 1 + 127, 0) - down, 1)
    scale = np.exp2(byte - 127.0)
    codes = (blocks / scale).astype(np.float32).astype(dtype).astype(np.float64)
    return np.moveaxis((codes * scale).reshape(v.shape), -1, axis)


WIDE = False


def mx_kscale(k):
    if not WIDE:
        return np.ones(k)
    levels = np.array([10, -10, 5, -5, 0])
    if k % 512:
        return np.exp2(np.random.permutation(np.resize(levels, k // 32))).repeat(32)
    a = np.empty((k // 512, 16))
    for p in range(k // 512):
        a[p, :8] = np.random.permutation(np.resize(levels, 8))
        for g in range(8):
            far = levels[np.abs(levels - a[p, g]) >= 10]
            a[p, g + 8] = far[np.random.randint(len(far))]
    return np.exp2(a.ravel()).repeat(32)


def f64(x):
    return np.asarray(x).astype(np.float64)


def striped(idx):
    return np.tile(idx.reshape(-1, 16).T, (8, 1)).astype(np.uint16)


def unstriped(offs):
    return offs[:16].T.reshape(-1).astype(np.int64)


def striped8(idx):
    return np.concatenate([x.reshape(-1, 16).T for x in idx]).astype(np.uint16)


def runs(offs, k):
    lists = np.stack([offs[16 * r : 16 * r + 16].T.reshape(-1) for r in range(8)]).astype(np.int64)
    return lists[np.arange(k) % 512 // 64]


def pack_weight(w):
    k, n = w.shape
    w = f64(np.asarray(w, np.float32).astype(ml_dtypes.bfloat16)).reshape(k // 32, 32, n)
    amax = np.abs(w).max(1)
    byte = np.clip(np.where(amax > 0, np.frexp(amax)[1] - 1 + 127 - 7, 1), 1, 254)
    scaled = (w * np.exp2(127.0 - byte)[:, None, :]).reshape(k, n).astype(np.float32)
    words = np.ascontiguousarray(scaled.reshape(k // 512, 128, 4, n).transpose(0, 1, 3, 2)).astype(ml_dtypes.float8_e4m3fn).view(np.uint8)
    return words, np.ascontiguousarray(byte.astype(np.uint8).reshape(k // 512, 16, n))


def unpack_weight(words, scales):
    g, p, n, _ = words.shape
    vals = np.ascontiguousarray(words).view(ml_dtypes.float8_e4m3fn).astype(np.float64) * np.repeat(np.exp2(scales.astype(np.float64) - 127.0), 8, axis=1)[..., None]
    return vals.transpose(0, 1, 3, 2).reshape(g * 512, n)


E2M1 = np.array([0.0, 0.5, 1.0, 1.5, 2.0, 3.0, 4.0, 6.0, -0.0, -0.5, -1.0, -1.5, -2.0, -3.0, -4.0, -6.0])


def pack_fp4(w):
    k, n = w.shape
    w = f64(np.asarray(w, np.float32).astype(ml_dtypes.bfloat16)).reshape(k // 32, 32, n)
    amax = np.abs(w).max(1)
    mant, ex = np.frexp(amax / 6.0)
    byte = np.clip(np.where(amax > 0, np.where(mant > 0.5, ex, ex - 1) + 127, 1), 1, 254)
    scaled = (w * np.exp2(127.0 - byte)[:, None, :]).reshape(k, n).astype(np.float32)
    c = np.ascontiguousarray(scaled.reshape(k // 512, 128, 4, n).transpose(0, 1, 3, 2)).astype(ml_dtypes.float4_e2m1fn).view(np.uint8) & 0xF
    words = (c[..., 0::2] | (c[..., 1::2] << 4)).reshape(k // 512, 128, 2 * n)
    return np.ascontiguousarray(words), np.ascontiguousarray(byte.astype(np.uint8).reshape(k // 512, 16, n))


def unpack_fp4(words, scales):
    g, _, n = scales.shape
    words = np.ascontiguousarray(words).reshape(g, 128, n, 2)
    nib = np.empty((g, 128, n, 4), np.uint8)
    nib[..., 0::2] = words & 0xF
    nib[..., 1::2] = words >> 4
    vals = E2M1[nib] * np.repeat(np.exp2(scales.astype(np.float64) - 127.0), 8, axis=1)[..., None]
    return vals.transpose(0, 1, 3, 2).reshape(g * 512, n)


def planes(y):
    n, m = y.shape
    v = y.astype(np.float32).astype(ml_dtypes.bfloat16).astype(np.float64).reshape(n // 32, 32, m)
    top = np.abs(v).max(1)
    byte = np.clip(np.where(top > 0, np.frexp(top)[1] - 1 + 127 - 7, 1), 1, 254)
    codes = (v * np.exp2(127.0 - byte)[:, None, :]).reshape(n, m).astype(np.float32).astype(ml_dtypes.float8_e4m3fn).view(np.uint8)
    words = codes.reshape(n // 512, 128, 4, m).transpose(0, 1, 3, 2)
    return np.ascontiguousarray(words), np.ascontiguousarray(byte.astype(np.uint8).reshape(n // 512, 16, m))


K, T, S, H, J, G = 512, 2048, 512, 512, 512, 2048


def setup_inputs():
    n = np.random.standard_normal
    s = mx_kscale(K)[:, None]
    packed_xT = pack_weight(n((K, T)) * s)
    packed_w1 = pack_fp4(n((K, H)) / np.sqrt(K) / s)
    packed_dT = pack_weight(n((K, G)) / s)
    return {
        "x_words": packed_xT[0],
        "x_scales": packed_xT[1],
        "w1_words": packed_w1[0],
        "w1_scales": packed_w1[1],
        "tab": n((H, J)).astype(np.float32),
        "gs": (np.random.uniform(0.5, 1.5, (K, 1)) * s).astype(np.float32),
        "d_words": packed_dT[0],
        "d_scales": packed_dT[1],
        "offs": striped(np.random.permutation(T)[:S]),
        "n1": striped8(np.random.randint(0, J, (8, S))),
        "n2": striped8(np.stack([np.random.permutation(S) for _ in range(8)])),
        "k1": striped8(np.random.randint(0, G, (8, H))),
        "n3": striped8(np.stack([np.random.permutation(S) for _ in range(8)])),
    }


def reference(x_words, x_scales, w1_words, w1_scales, tab, gs, d_words, d_scales, offs, n1, n2, k1, n3):
    d_k1 = unpack_weight(d_words, d_scales)[np.arange(K)[:, None], runs(k1, K)]
    xq = unpack_weight(x_words, x_scales)[:, unstriped(offs)]
    y = unpack_fp4(w1_words, w1_scales).T @ xq
    z = f64(gs) * (np.abs(y - (y[np.arange(H)[:, None], runs(n2, H)]) - (f64(tab)[np.arange(H)[:, None], runs(n1, H)])))
    h = 0.0625 * ((d_k1.T @ mxq(z, 0, "e4m3")))
    out_0 = h / (np.abs(h[np.arange(H)[:, None], runs(n3, H)]) + 0.5)
    return (out_0,) + planes(out_0)

@@ -1,0 +1,241 @@
+from contextlib import ExitStack
+
+import concourse.mybir as mybir
+
+K, T, S, H, J, G = 512, 2048, 512, 512, 512, 2048
+FLOPS = 2 * K * H * S + 2 * H * H * S
+
+F32 = mybir.dt.float32
+BF16 = mybir.dt.bfloat16
+I32 = mybir.dt.int32
+U32 = mybir.dt.uint32
+U16 = mybir.dt.uint16
+U8 = mybir.dt.uint8
+FP8X4 = mybir.dt.float8_e4m3fn_x4
+FP4X4 = mybir.dt.float4_e2m1fn_x4
+ACT = mybir.ActivationFunctionType
+ALU = mybir.AluOpType
+
+P = 128
+PACK = 4
+N = 128
+STRIPS = S // N
+OUT_CHUNKS = ((0, 256), (256, 128), (384, 128))
+
+
+def tile_picked_densekinddnorm_none_po_kernel(
+    tc, x_words, x_scales, w1_words, w1_scales, tab, gs, d_words, d_scales, offs, n1, n2, k1, n3, out_0, out_1, out_2
+):
+    nc = tc.nc
+    with ExitStack() as ctx:
+        lists = ctx.enter_context(tc.tile_pool(name="lists", bufs=1))
+        sb = ctx.enter_context(tc.tile_pool(name="sb", bufs=1))
+        placed = ctx.enter_context(tc.tile_pool(name="placed", bufs=1))
+        ps = ctx.enter_context(tc.psum_pool(name="ps", bufs=1))
+
+        def sbuf(name, shape, dtype, tag=None):
+            return sb.tile(shape, dtype, name=name, tag=tag or name, align_bytes=64)
+
+        def place(name, shape, dtype, offset):
+            return placed.tile(shape, dtype, name=name, align_bytes=64, offset=offset)
+
+        offs_t = lists.tile([P, S // 16], U16, name="offs_t")
+        k1_t = lists.tile([P, H // 16], U16, name="k1_t")
+        n1_t = lists.tile([P, S // 16], U16, name="n1_t")
+        n2_t = lists.tile([P, S // 16], U16, name="n2_t")
+        n3_t = lists.tile([P, S // 16], U16, name="n3_t")
+
+        xw = place("xw", [P, T], U32, 512)
+        xs = place("xs", [P, T], U8, 8704)
+        ds = sbuf("ds", [P, G], U8)
+        w1_raw = place("w1_raw", [P, 2 * H], U8, 12288)
+        w1s_raw = place("w1s_raw", [P, H], U8, 20480)
+        d_plane = sbuf("d_plane", [P, H], U8)
+        gs_t = sbuf("gs_t", [P, PACK], F32)
+
+        warm = sbuf("warm", [P, 1], F32)
+        nc.vector.memset(warm[:], 1.0)
+        nc.vector.memset(xs[:].bitcast(I32), 0)
+        nc.vector.memset(w1s_raw[:].bitcast(I32), 0)
+        nc.vector.memset(d_plane[:].bitcast(I32), 0)
+        warm_out = sbuf("warm_out", [P, 1], F32)
+        nc.scalar.activation(warm_out[:], warm[:], ACT.Abs_reciprocal_sqrt)
+
+        nc.gpsimd.memset(ds[:].bitcast(I32), 0)
+        nc.gpsimd.dma_start(ds[0:P:8, :].bitcast(I32), d_scales[0].bitcast(I32))
+
+        nc.sync.dma_start(offs_t[:], offs)
+        nc.sync.dma_start(w1_raw[:].bitcast(I32), w1_words[0].bitcast(I32))
+        nc.sync.dma_start(k1_t[:], k1)
+        nc.sync.dma_start(n1_t[:], n1)
+        nc.sync.dma_start(n2_t[:], n2)
+        nc.sync.dma_start(n3_t[:], n3)
+        nc.sync.dma_start(xw[:].bitcast(I32), x_words[0].rearrange("p n t -> p (n t)").bitcast(I32))
+        for a in range(PACK):
+            nc.scalar.dma_start(xs[a:P:32, :].bitcast(I32), x_scales[0, a:16:4, :].bitcast(I32))
+        for a in range(PACK):
+            nc.scalar.dma_start(w1s_raw[a:P:32, :].bitcast(I32), w1_scales[0, a:16:4, :].bitcast(I32))
+        nc.gpsimd.dma_start(gs_t[:], gs.rearrange("(p t) o -> p (t o)", t=PACK))
+
+        w1_w = sbuf("w1_w", [P, 2 * H], U8)
+        nc.vector.tensor_copy(
+            w1_w[:].rearrange("p (t m b) -> p t m b", t=PACK, b=2),
+            w1_raw[:].rearrange("p (m t b) -> p t m b", t=PACK, b=2),
+        )
+        dw = place("dw", [P, G], U32, 12288)
+        nc.sync.dma_start(dw[:].bitcast(I32), d_words[0].rearrange("p n t -> p (n t)").bitcast(I32))
+        xq_w = sbuf("xq_w", [P, S], U32)
+        nc.vector.tensor_copy(xq_w[:], xw[:].indirect(offs_t[:]))
+        xq_s = sbuf("xq_s", [P, S], U8)
+        nc.vector.tensor_copy(xq_s[:], xs[:].indirect(offs_t[:]))
+        w1_s = place("w1_s", [P, H], U8, 8448)
+        nc.vector.tensor_copy(
+            w1_s[:].rearrange("p (t m) -> p t m", t=PACK), w1s_raw[:].rearrange("p (m t) -> p t m", t=PACK)
+        )
+
+        tab_rows = tab.rearrange("(p t) c -> p t c", t=PACK)
+        tabs = []
+        for t in range(PACK):
+            tab_t = place("tab%d" % t, [P, J], F32, 2048 * t)
+            nc.sync.dma_start(tab_t[:], tab_rows[:, t, :])
+            tabs.append(tab_t)
+
+        ys = []
+        for t in range(PACK):
+            y_ps = ps.tile([P, S], F32, name="y_ps%d" % t, tag="plane%d" % t)
+            nc.tensor.matmul_mx(
+                out=y_ps[:],
+                lhsT=w1_w[:, 2 * P * t : 2 * P * (t + 1)].bitcast(FP4X4),
+                lhsT_scale=w1_s[:, P * t : P * (t + 1)],
+                rhs=xq_w[:].bitcast(FP8X4),
+                rhs_scale=xq_s[:],
+                start=True,
+                stop=True,
+            )
+            y = sbuf("y%d" % t, [P, S], F32)
+            nc.scalar.copy(y[:], y_ps[:])
+            ys.append(y)
+
+        dq_s = sbuf("dq_s", [P, H], U8)
+        nc.vector.tensor_copy(dq_s[:], ds[:].indirect(k1_t[:]))
+        dq_w = place("dq_w", [P, H], U32, 20480)
+        nc.vector.tensor_copy(dq_w[:], dw[:].indirect(k1_t[:]))
+        dealt_s = sbuf("dealt_s", [P, H], U8)
+        nc.vector.tensor_copy(
+            dealt_s[:].rearrange("p (t m) -> p t m", t=PACK), dq_s[:].rearrange("p (m t) -> p t m", t=PACK)
+        )
+        for a in range(PACK):
+            nc.sync.dma_start(d_plane[a:P:32, :].bitcast(I32), dealt_s[8 * a : P : 32, :].bitcast(I32))
+        d_w = sbuf("d_w", [P, H], U32)
+        nc.vector.tensor_copy(
+            d_w[:].bitcast(I32).rearrange("p (t m) -> p t m", t=PACK),
+            dq_w[:].bitcast(I32).rearrange("p (m t) -> p t m", t=PACK),
+        )
+
+        recips = [sbuf("recip%d" % t, [P, S], F32) for t in range(PACK)]
+
+        def columns(c):
+            return slice(N * c, N * (c + 1))
+
+        def entries(c):
+            return slice(N * c // 16, N * (c + 1) // 16)
+
+        def table_less_y(c):
+            us = [sbuf("u%d_%d" % (c, t), [P, N], F32, tag="u%d" % t) for t in range(PACK)]
+            for t in range(PACK):
+                nc.vector.tensor_tensor(
+                    us[t][:], tabs[t][:].indirect(n1_t[:, entries(c)]), ys[t][:, columns(c)], ALU.subtract
+                )
+            return us
+
+        def weave(c, z):
+            woven = sbuf("z_woven%d" % c, [P, N, PACK], BF16)
+            nc.vector.tensor_copy(woven[:], z[:].rearrange("p t c -> p c t"))
+            return woven
+
+        def quantise(c, woven):
+            z_w = sbuf("z_w%d" % c, [P, N], U32)
+            z_s = sbuf("z_s%d" % c, [P, N], U8)
+            nc.vector.quantize_mx(out=z_w[:].bitcast(FP8X4), scales=z_s[:], in_=woven[:].rearrange("p c t -> p (c t)"))
+            return z_w, z_s
+
+        def product(out, t, z_w, z_s):
+            nc.tensor.matmul_mx(
+                out=out,
+                lhsT=d_w[:, P * t : P * (t + 1)].bitcast(FP8X4),
+                lhsT_scale=d_plane[:, P * t : P * (t + 1)],
+                rhs=z_w[:].bitcast(FP8X4),
+                rhs_scale=z_s[:],
+                start=True,
+                stop=True,
+            )
+
+        def inverse_roots(name, shape, h_ps):
+            h_size = sbuf("h_size" + name, shape, F32)
+            nc.scalar.activation(h_size[:], h_ps, ACT.Abs, scale=0.0625)
+            root = sbuf("root" + name, shape, F32)
+            nc.scalar.activation(root[:], h_size[:], ACT.Abs_reciprocal_sqrt, bias=0.5)
+            return root
+
+        h_banks = []
+        z_prev = None
+        for c in range(STRIPS):
+            us = table_less_y(c)
+            if c > 0:
+                woven = weave(c - 1, z_prev)
+            g = sbuf("g%d" % c, [P, PACK, N], F32, tag="z%d" % (c - 1))
+            size = sbuf("size%d" % c, [P, PACK, N], F32)
+            z = sbuf("z%d" % c, [P, PACK, N], BF16)
+            for t in range(PACK):
+                nc.vector.tensor_tensor(g[:, t, :], ys[t][:].indirect(n2_t[:, entries(c)]), us[t][:], ALU.add)
+                if c > 0 and t == 0:
+                    z_w, z_s = quantise(c - 1, woven)
+                nc.scalar.activation(size[:, t, :], g[:, t, :], ACT.Abs)
+                nc.scalar.activation(z[:, t, :], size[:, t, :], ACT.Copy, scale=gs_t[:, t : t + 1])
+            if c > 0:
+                h_ps = ps.tile([P, PACK, N], F32, name="h_ps%d" % (c - 1))
+                for t in range(PACK):
+                    product(h_ps[:, t, :], t, z_w, z_s)
+                root = inverse_roots("%d" % (c - 1), [P, PACK, N], h_ps[:])
+                for t in range(PACK):
+                    nc.scalar.activation(recips[t][:, columns(c - 1)], root[:, t, :], ACT.Square)
+                h_banks.append(h_ps)
+            z_prev = z
+
+        last = STRIPS - 1
+        woven = weave(last, z_prev)
+        z_w, z_s = quantise(last, woven)
+        h = sbuf("h", [P, PACK, S], F32, tag="z_woven%d" % last)
+        h_last = []
+        for t in range(PACK):
+            h_ps = ps.tile([P, N], F32, name="h_last%d" % t, tag="plane%d" % t)
+            product(h_ps[:], t, z_w, z_s)
+            root = inverse_roots("_last%d" % t, [P, N], h_ps[:])
+            nc.scalar.activation(recips[t][:, columns(last)], root[:], ACT.Square)
+            h_last.append(h_ps)
+        for c in range(last):
+            nc.vector.tensor_scalar(h[:, :, columns(c)], h_banks[c][:], 0.0625, None, ALU.mult)
+        for t in range(PACK):
+            nc.scalar.activation(h[:, t, columns(last)], h_last[t][:], ACT.Copy, scale=0.0625)
+
+        out_rows = out_0.rearrange("(p t) c -> p t c", t=PACK)
+        out_s = sbuf("out_s", [P, S], U8)
+        word_rows = out_1[0].rearrange("p n t -> p (n t)").bitcast(I32)
+        for c0, n in OUT_CHUNKS:
+            cols = slice(c0, c0 + n)
+            res = sbuf("res%d" % c0, [P, PACK, n], F32)
+            for t in range(PACK):
+                nc.vector.tensor_tensor(
+                    res[:, t, :], recips[t][:].indirect(n3_t[:, c0 // 16 : (c0 + n) // 16]), h[:, t, cols], ALU.mult
+                )
+            nc.sync.dma_start(out_rows[:, :, cols], res[:])
+            woven = sbuf("res_woven%d" % c0, [P, n, PACK], BF16)
+            nc.scalar.copy(woven[:], res[:].rearrange("p t c -> p c t"))
+            out_w = sbuf("out_w%d" % c0, [P, n], U32)
+            nc.vector.quantize_mx(
+                out=out_w[:].bitcast(FP8X4), scales=out_s[:, cols], in_=woven[:].rearrange("p c t -> p (c t)")
+            )
+            nc.sync.dma_start(word_rows[:, cols], out_w[:].bitcast(I32))
+        for a in range(PACK):
+            queue = nc.sync if a % 2 == 0 else nc.scalar
+            queue.dma_start(out_2[0, a:16:4, :].bitcast(I32), out_s[a:P:32, :].bitcast(I32))

@@ -30,14 +30,10 @@ def tile_picked_densekinddnorm_none_po_kernel(
     with ExitStack() as ctx:
         lists = ctx.enter_context(tc.tile_pool(name="lists", bufs=1))
         sb = ctx.enter_context(tc.tile_pool(name="sb", bufs=1))
-        placed = ctx.enter_context(tc.tile_pool(name="placed", bufs=1))
         ps = ctx.enter_context(tc.psum_pool(name="ps", bufs=1))
 
         def sbuf(name, shape, dtype, tag=None):
             return sb.tile(shape, dtype, name=name, tag=tag or name, align_bytes=64)
-
-        def place(name, shape, dtype, offset):
-            return placed.tile(shape, dtype, name=name, align_bytes=64, offset=offset)
 
         offs_t = lists.tile([P, S // 16], U16, name="offs_t")
         k1_t = lists.tile([P, H // 16], U16, name="k1_t")
@@ -45,60 +41,61 @@ def tile_picked_densekinddnorm_none_po_kernel(
         n2_t = lists.tile([P, S // 16], U16, name="n2_t")
         n3_t = lists.tile([P, S // 16], U16, name="n3_t")
 
-        xw = place("xw", [P, T], U32, 512)
-        xs = place("xs", [P, T], U8, 8704)
+        xw = sbuf("xw", [P, T], U32)
+        xs = sbuf("xs", [P, T], U8)
         ds = sbuf("ds", [P, G], U8)
-        w1_raw = place("w1_raw", [P, 2 * H], U8, 12288)
-        w1s_raw = place("w1s_raw", [P, H], U8, 20480)
+        w1_raw = sbuf("w1_raw", [P, 2 * H], U8)
+        w1s_raw = sbuf("w1s_raw", [P, H], U8)
         d_plane = sbuf("d_plane", [P, H], U8)
-        gs_t = sbuf("gs_t", [P, PACK], F32)
 
+        nc.gpsimd.memset(xs[:].bitcast(I32), 0)
+        nc.gpsimd.memset(ds[:].bitcast(I32), 0)
+        nc.gpsimd.memset(d_plane[:].bitcast(I32), 0)
+        nc.vector.memset(w1s_raw[:].bitcast(I32), 0)
         warm = sbuf("warm", [P, 1], F32)
         nc.vector.memset(warm[:], 1.0)
-        nc.vector.memset(xs[:].bitcast(I32), 0)
-        nc.vector.memset(w1s_raw[:].bitcast(I32), 0)
-        nc.vector.memset(d_plane[:].bitcast(I32), 0)
         warm_out = sbuf("warm_out", [P, 1], F32)
         nc.scalar.activation(warm_out[:], warm[:], ACT.Abs_reciprocal_sqrt)
 
-        nc.gpsimd.memset(ds[:].bitcast(I32), 0)
-        nc.gpsimd.dma_start(ds[0:P:8, :].bitcast(I32), d_scales[0].bitcast(I32))
-
-        nc.sync.dma_start(offs_t[:], offs)
         nc.sync.dma_start(w1_raw[:].bitcast(I32), w1_words[0].bitcast(I32))
-        nc.sync.dma_start(k1_t[:], k1)
-        nc.sync.dma_start(n1_t[:], n1)
-        nc.sync.dma_start(n2_t[:], n2)
-        nc.sync.dma_start(n3_t[:], n3)
+        nc.sync.dma_start(offs_t[:], offs)
+        for a in range(PACK):
+            nc.sync.dma_start(xs[a:P:32, :].bitcast(I32), x_scales[0, a:16:4, :].bitcast(I32))
         nc.sync.dma_start(xw[:].bitcast(I32), x_words[0].rearrange("p n t -> p (n t)").bitcast(I32))
         for a in range(PACK):
-            nc.scalar.dma_start(xs[a:P:32, :].bitcast(I32), x_scales[0, a:16:4, :].bitcast(I32))
-        for a in range(PACK):
-            nc.scalar.dma_start(w1s_raw[a:P:32, :].bitcast(I32), w1_scales[0, a:16:4, :].bitcast(I32))
-        nc.gpsimd.dma_start(gs_t[:], gs.rearrange("(p t) o -> p (t o)", t=PACK))
+            nc.sync.dma_start(w1s_raw[a:P:32, :].bitcast(I32), w1_scales[0, a:16:4, :].bitcast(I32))
+        nc.sync.dma_start(k1_t[:], k1)
+        nc.sync.dma_start(ds[0:P:8, :].bitcast(I32), d_scales[0].bitcast(I32))
 
-        w1_w = sbuf("w1_w", [P, 2 * H], U8)
-        nc.vector.tensor_copy(
-            w1_w[:].rearrange("p (t m b) -> p t m b", t=PACK, b=2),
-            w1_raw[:].rearrange("p (m t b) -> p t m b", t=PACK, b=2),
-        )
-        dw = place("dw", [P, G], U32, 12288)
+        dw = sbuf("dw", [P, G], U32)
         nc.sync.dma_start(dw[:].bitcast(I32), d_words[0].rearrange("p n t -> p (n t)").bitcast(I32))
-        xq_w = sbuf("xq_w", [P, S], U32)
-        nc.vector.tensor_copy(xq_w[:], xw[:].indirect(offs_t[:]))
-        xq_s = sbuf("xq_s", [P, S], U8)
-        nc.vector.tensor_copy(xq_s[:], xs[:].indirect(offs_t[:]))
-        w1_s = place("w1_s", [P, H], U8, 8448)
-        nc.vector.tensor_copy(
-            w1_s[:].rearrange("p (t m) -> p t m", t=PACK), w1s_raw[:].rearrange("p (m t) -> p t m", t=PACK)
-        )
-
+        nc.sync.dma_start(n1_t[:], n1)
+        nc.sync.dma_start(n2_t[:], n2)
         tab_rows = tab.rearrange("(p t) c -> p t c", t=PACK)
         tabs = []
         for t in range(PACK):
-            tab_t = place("tab%d" % t, [P, J], F32, 2048 * t)
+            tab_t = sbuf("tab%d" % t, [P, J], F32)
             nc.sync.dma_start(tab_t[:], tab_rows[:, t, :])
             tabs.append(tab_t)
+
+        gs_t = sbuf("gs_t", [P, PACK], F32)
+        nc.sync.dma_start(gs_t[:], gs.rearrange("(p t) o -> p (t o)", t=PACK))
+        nc.sync.dma_start(n3_t[:], n3)
+
+        w1_w = sbuf("w1_w", [P, 2 * H], U8)
+        nc.vector.tensor_copy(
+            w1_w[:].rearrange("p (t m i b) -> p m t i b", t=PACK, i=8, b=2),
+            w1_raw[:].rearrange("p (m i t b) -> p m t i b", t=PACK, i=8, b=2),
+        )
+        xq_s = sbuf("xq_s", [P, S], U8)
+        nc.vector.tensor_copy(xq_s[:], xs[:].indirect(offs_t[:]))
+        xq_w = sbuf("xq_w", [P, S], U32)
+        nc.vector.tensor_copy(xq_w[:], xw[:].indirect(offs_t[:]))
+        w1_s = sbuf("w1_s", [P, H], U8)
+        nc.vector.tensor_copy(
+            w1_s[:].rearrange("p (t m i) -> p m t i", t=PACK, i=16),
+            w1s_raw[:].rearrange("p (m i t) -> p m t i", t=PACK, i=16),
+        )
 
         ys = []
         for t in range(PACK):
@@ -116,23 +113,26 @@ def tile_picked_densekinddnorm_none_po_kernel(
             nc.scalar.copy(y[:], y_ps[:])
             ys.append(y)
 
-        dq_s = sbuf("dq_s", [P, H], U8)
+        dq_s = sbuf("dq_s", [P, H], U8, tag="xw")
         nc.vector.tensor_copy(dq_s[:], ds[:].indirect(k1_t[:]))
-        dq_w = place("dq_w", [P, H], U32, 20480)
+        dq_w = sbuf("dq_w", [P, H], U32)
         nc.vector.tensor_copy(dq_w[:], dw[:].indirect(k1_t[:]))
         dealt_s = sbuf("dealt_s", [P, H], U8)
         nc.vector.tensor_copy(
-            dealt_s[:].rearrange("p (t m) -> p t m", t=PACK), dq_s[:].rearrange("p (m t) -> p t m", t=PACK)
+            dealt_s[:].rearrange("p (t m i) -> p m t i", t=PACK, i=16),
+            dq_s[:].rearrange("p (m i t) -> p m t i", t=PACK, i=16),
         )
         for a in range(PACK):
             nc.sync.dma_start(d_plane[a:P:32, :].bitcast(I32), dealt_s[8 * a : P : 32, :].bitcast(I32))
         d_w = sbuf("d_w", [P, H], U32)
-        nc.vector.tensor_copy(
-            d_w[:].bitcast(I32).rearrange("p (t m) -> p t m", t=PACK),
-            dq_w[:].bitcast(I32).rearrange("p (m t) -> p t m", t=PACK),
-        )
 
         recips = [sbuf("recip%d" % t, [P, S], F32) for t in range(PACK)]
+
+        def weaving(woven, planes):
+            return (
+                woven[:].rearrange("p (c i) t -> p c t i", i=4),
+                planes[:].rearrange("p t (c i) -> p c t i", i=4),
+            )
 
         def columns(c):
             return slice(N * c, N * (c + 1))
@@ -150,7 +150,7 @@ def tile_picked_densekinddnorm_none_po_kernel(
 
         def weave(c, z):
             woven = sbuf("z_woven%d" % c, [P, N, PACK], BF16)
-            nc.vector.tensor_copy(woven[:], z[:].rearrange("p t c -> p c t"))
+            nc.vector.tensor_copy(*weaving(woven, z))
             return woven
 
         def quantise(c, woven):
@@ -170,67 +170,88 @@ def tile_picked_densekinddnorm_none_po_kernel(
                 stop=True,
             )
 
-        def inverse_roots(name, shape, h_ps):
-            h_size = sbuf("h_size" + name, shape, F32)
+        def inverse_roots(name, root, h_ps):
+            h_size = sbuf("h_size" + name, list(root.shape), F32)
             nc.scalar.activation(h_size[:], h_ps, ACT.Abs, scale=0.0625)
-            root = sbuf("root" + name, shape, F32)
-            nc.scalar.activation(root[:], h_size[:], ACT.Abs_reciprocal_sqrt, bias=0.5)
-            return root
+            nc.scalar.activation(root, h_size[:], ACT.Abs_reciprocal_sqrt, bias=0.5)
+
+        last = STRIPS - 1
+        late_roots = sbuf("late_roots", [P, PACK, 2 * N], F32)
 
         h_banks = []
         z_prev = None
         for c in range(STRIPS):
             us = table_less_y(c)
+            if c == 0:
+                nc.vector.tensor_copy(
+                    d_w[:].bitcast(I32).rearrange("p (t m i) -> p m t i", t=PACK, i=4),
+                    dq_w[:].bitcast(I32).rearrange("p (m i t) -> p m t i", t=PACK, i=4),
+                )
             if c > 0:
                 woven = weave(c - 1, z_prev)
-            g = sbuf("g%d" % c, [P, PACK, N], F32, tag="z%d" % (c - 1))
+            g = sbuf("g%d" % c, [P, PACK, N], F32, tag="size%d" % (c - 1))
             size = sbuf("size%d" % c, [P, PACK, N], F32)
             z = sbuf("z%d" % c, [P, PACK, N], BF16)
             for t in range(PACK):
                 nc.vector.tensor_tensor(g[:, t, :], ys[t][:].indirect(n2_t[:, entries(c)]), us[t][:], ALU.add)
                 if c > 0 and t == 0:
                     z_w, z_s = quantise(c - 1, woven)
-                nc.scalar.activation(size[:, t, :], g[:, t, :], ACT.Abs)
-                nc.scalar.activation(z[:, t, :], size[:, t, :], ACT.Copy, scale=gs_t[:, t : t + 1])
+                if c == last:
+                    nc.scalar.activation(size[:, t, :], g[:, t, :], ACT.Abs)
+                    nc.scalar.activation(z[:, t, :], size[:, t, :], ACT.Copy, scale=gs_t[:, t : t + 1])
+                elif t % 2 == 1:
+                    nc.scalar.activation(size[:, t - 1 : t + 1, :], g[:, t - 1 : t + 1, :], ACT.Abs)
+                    for r in (t - 1, t):
+                        nc.scalar.activation(z[:, r, :], size[:, r, :], ACT.Copy, scale=gs_t[:, r : r + 1])
             if c > 0:
                 h_ps = ps.tile([P, PACK, N], F32, name="h_ps%d" % (c - 1))
                 for t in range(PACK):
                     product(h_ps[:, t, :], t, z_w, z_s)
-                root = inverse_roots("%d" % (c - 1), [P, PACK, N], h_ps[:])
-                for t in range(PACK):
-                    nc.scalar.activation(recips[t][:, columns(c - 1)], root[:, t, :], ACT.Square)
+                if c == last:
+                    inverse_roots("%d" % (c - 1), late_roots[:, :, 0:N], h_ps[:])
+                else:
+                    root = sbuf("root%d" % (c - 1), [P, PACK, N], F32)
+                    inverse_roots("%d" % (c - 1), root[:], h_ps[:])
+                    for t in range(PACK):
+                        nc.scalar.activation(recips[t][:, columns(c - 1)], root[:, t, :], ACT.Square)
                 h_banks.append(h_ps)
             z_prev = z
 
-        last = STRIPS - 1
         woven = weave(last, z_prev)
         z_w, z_s = quantise(last, woven)
-        h = sbuf("h", [P, PACK, S], F32, tag="z_woven%d" % last)
         h_last = []
         for t in range(PACK):
             h_ps = ps.tile([P, N], F32, name="h_last%d" % t, tag="plane%d" % t)
             product(h_ps[:], t, z_w, z_s)
-            root = inverse_roots("_last%d" % t, [P, N], h_ps[:])
-            nc.scalar.activation(recips[t][:, columns(last)], root[:], ACT.Square)
+            inverse_roots("_last%d" % t, late_roots[:, t, N : 2 * N], h_ps[:])
+            nc.scalar.activation(recips[t][:, 2 * N : 4 * N], late_roots[:, t, :], ACT.Square)
             h_last.append(h_ps)
-        for c in range(last):
-            nc.vector.tensor_scalar(h[:, :, columns(c)], h_banks[c][:], 0.0625, None, ALU.mult)
+        h_early = sbuf("h_early", [P, PACK, 2 * N], F32, tag="z_woven%d" % last)
+        for c in range(2):
+            nc.vector.tensor_scalar(h_early[:, :, columns(c)], h_banks[c][:], 0.0625, None, ALU.mult)
+        h_late = sbuf("h_late", [P, PACK, 2 * N], F32, tag="late_roots")
+        nc.scalar.activation(h_late[:, :, 0:N], h_banks[2][:], ACT.Copy, scale=0.0625)
         for t in range(PACK):
-            nc.scalar.activation(h[:, t, columns(last)], h_last[t][:], ACT.Copy, scale=0.0625)
+            nc.scalar.activation(h_late[:, t, N : 2 * N], h_last[t][:], ACT.Copy, scale=0.0625)
 
         out_rows = out_0.rearrange("(p t) c -> p t c", t=PACK)
         out_s = sbuf("out_s", [P, S], U8)
         word_rows = out_1[0].rearrange("p n t -> p (n t)").bitcast(I32)
         for c0, n in OUT_CHUNKS:
             cols = slice(c0, c0 + n)
+            h = h_early if c0 < 2 * N else h_late
+            h_cols = slice(c0 % (2 * N), c0 % (2 * N) + n)
             res = sbuf("res%d" % c0, [P, PACK, n], F32)
             for t in range(PACK):
                 nc.vector.tensor_tensor(
-                    res[:, t, :], recips[t][:].indirect(n3_t[:, c0 // 16 : (c0 + n) // 16]), h[:, t, cols], ALU.mult
+                    res[:, t, :], recips[t][:].indirect(n3_t[:, c0 // 16 : (c0 + n) // 16]), h[:, t, h_cols], ALU.mult
                 )
             nc.sync.dma_start(out_rows[:, :, cols], res[:])
             woven = sbuf("res_woven%d" % c0, [P, n, PACK], BF16)
-            nc.scalar.copy(woven[:], res[:].rearrange("p t c -> p c t"))
+            if c0 + n < S:
+                nc.scalar.copy(*weaving(woven, res))
+            else:
+                nc.vector.tensor_copy(*weaving(woven, res))
             out_w = sbuf("out_w%d" % c0, [P, n], U32)
             nc.vector.quantize_mx(
                 out=out_w[:].bitcast(FP8X4), scales=out_s[:, cols], in_=woven[:].rearrange("p c t -> p (c t)")

from contextlib import ExitStack

import concourse.mybir as mybir

K, T, S, H, J, G = 512, 2048, 512, 512, 512, 2048
FLOPS = 2 * K * H * S + 2 * H * H * S

F32 = mybir.dt.float32
BF16 = mybir.dt.bfloat16
I32 = mybir.dt.int32
U32 = mybir.dt.uint32
U16 = mybir.dt.uint16
U8 = mybir.dt.uint8
FP8X4 = mybir.dt.float8_e4m3fn_x4
FP4X4 = mybir.dt.float4_e2m1fn_x4
ACT = mybir.ActivationFunctionType
ALU = mybir.AluOpType

P = 128
PACK = 4
N = 128
STRIPS = S // N
OUT_CHUNKS = ((0, 256), (256, 128), (384, 128))


def tile_picked_densekinddnorm_none_po_kernel(
    tc, x_words, x_scales, w1_words, w1_scales, tab, gs, d_words, d_scales, offs, n1, n2, k1, n3, out_0, out_1, out_2
):
    nc = tc.nc
    with ExitStack() as ctx:
        lists = ctx.enter_context(tc.tile_pool(name="lists", bufs=1))
        sb = ctx.enter_context(tc.tile_pool(name="sb", bufs=1))
        ps = ctx.enter_context(tc.psum_pool(name="ps", bufs=1))

        def sbuf(name, shape, dtype, tag=None):
            return sb.tile(shape, dtype, name=name, tag=tag or name, align_bytes=64)

        offs_t = lists.tile([P, S // 16], U16, name="offs_t")
        k1_t = lists.tile([P, H // 16], U16, name="k1_t")
        n1_t = lists.tile([P, S // 16], U16, name="n1_t")
        n2_t = lists.tile([P, S // 16], U16, name="n2_t")
        n3_t = lists.tile([P, S // 16], U16, name="n3_t")

        xw = sbuf("xw", [P, T], U32)
        xs = sbuf("xs", [P, T], U8)
        ds = sbuf("ds", [P, G], U8)
        w1_raw = sbuf("w1_raw", [P, 2 * H], U8)
        w1s_raw = sbuf("w1s_raw", [P, H], U8)
        d_plane = sbuf("d_plane", [P, H], U8)

        nc.gpsimd.memset(xs[:].bitcast(I32), 0)
        nc.gpsimd.memset(ds[:].bitcast(I32), 0)
        nc.gpsimd.memset(d_plane[:].bitcast(I32), 0)
        nc.vector.memset(w1s_raw[:].bitcast(I32), 0)
        warm = sbuf("warm", [P, 1], F32)
        nc.vector.memset(warm[:], 1.0)
        warm_out = sbuf("warm_out", [P, 1], F32)
        nc.scalar.activation(warm_out[:], warm[:], ACT.Abs_reciprocal_sqrt)

        nc.sync.dma_start(w1_raw[:].bitcast(I32), w1_words[0].bitcast(I32))
        nc.sync.dma_start(offs_t[:], offs)
        for a in range(PACK):
            nc.sync.dma_start(xs[a:P:32, :].bitcast(I32), x_scales[0, a:16:4, :].bitcast(I32))
        nc.sync.dma_start(xw[:].bitcast(I32), x_words[0].rearrange("p n t -> p (n t)").bitcast(I32))
        for a in range(PACK):
            nc.sync.dma_start(w1s_raw[a:P:32, :].bitcast(I32), w1_scales[0, a:16:4, :].bitcast(I32))
        nc.sync.dma_start(k1_t[:], k1)
        nc.sync.dma_start(ds[0:P:8, :].bitcast(I32), d_scales[0].bitcast(I32))

        dw = sbuf("dw", [P, G], U32)
        nc.sync.dma_start(dw[:].bitcast(I32), d_words[0].rearrange("p n t -> p (n t)").bitcast(I32))
        nc.sync.dma_start(n1_t[:], n1)
        nc.sync.dma_start(n2_t[:], n2)
        tab_rows = tab.rearrange("(p t) c -> p t c", t=PACK)
        tabs = []
        for t in range(PACK):
            tab_t = sbuf("tab%d" % t, [P, J], F32)
            nc.sync.dma_start(tab_t[:], tab_rows[:, t, :])
            tabs.append(tab_t)

        gs_t = sbuf("gs_t", [P, PACK], F32)
        nc.sync.dma_start(gs_t[:], gs.rearrange("(p t) o -> p (t o)", t=PACK))
        nc.sync.dma_start(n3_t[:], n3)

        w1_w = sbuf("w1_w", [P, 2 * H], U8)
        nc.vector.tensor_copy(
            w1_w[:].rearrange("p (t m i b) -> p m t i b", t=PACK, i=8, b=2),
            w1_raw[:].rearrange("p (m i t b) -> p m t i b", t=PACK, i=8, b=2),
        )
        xq_s = sbuf("xq_s", [P, S], U8)
        nc.vector.tensor_copy(xq_s[:], xs[:].indirect(offs_t[:]))
        xq_w = sbuf("xq_w", [P, S], U32)
        nc.vector.tensor_copy(xq_w[:], xw[:].indirect(offs_t[:]))
        w1_s = sbuf("w1_s", [P, H], U8)
        nc.vector.tensor_copy(
            w1_s[:].rearrange("p (t m i) -> p m t i", t=PACK, i=16),
            w1s_raw[:].rearrange("p (m i t) -> p m t i", t=PACK, i=16),
        )

        ys = []
        for t in range(PACK):
            y_ps = ps.tile([P, S], F32, name="y_ps%d" % t, tag="plane%d" % t)
            nc.tensor.matmul_mx(
                out=y_ps[:],
                lhsT=w1_w[:, 2 * P * t : 2 * P * (t + 1)].bitcast(FP4X4),
                lhsT_scale=w1_s[:, P * t : P * (t + 1)],
                rhs=xq_w[:].bitcast(FP8X4),
                rhs_scale=xq_s[:],
                start=True,
                stop=True,
            )
            y = sbuf("y%d" % t, [P, S], F32)
            nc.scalar.copy(y[:], y_ps[:])
            ys.append(y)

        dq_s = sbuf("dq_s", [P, H], U8, tag="xw")
        nc.vector.tensor_copy(dq_s[:], ds[:].indirect(k1_t[:]))
        dq_w = sbuf("dq_w", [P, H], U32)
        nc.vector.tensor_copy(dq_w[:], dw[:].indirect(k1_t[:]))
        dealt_s = sbuf("dealt_s", [P, H], U8)
        nc.vector.tensor_copy(
            dealt_s[:].rearrange("p (t m i) -> p m t i", t=PACK, i=16),
            dq_s[:].rearrange("p (m i t) -> p m t i", t=PACK, i=16),
        )
        for a in range(PACK):
            nc.sync.dma_start(d_plane[a:P:32, :].bitcast(I32), dealt_s[8 * a : P : 32, :].bitcast(I32))
        d_w = sbuf("d_w", [P, H], U32)

        recips = [sbuf("recip%d" % t, [P, S], F32) for t in range(PACK)]

        def weaving(woven, planes):
            return (
                woven[:].rearrange("p (c i) t -> p c t i", i=4),
                planes[:].rearrange("p t (c i) -> p c t i", i=4),
            )

        def columns(c):
            return slice(N * c, N * (c + 1))

        def entries(c):
            return slice(N * c // 16, N * (c + 1) // 16)

        def table_less_y(c):
            us = [sbuf("u%d_%d" % (c, t), [P, N], F32, tag="u%d" % t) for t in range(PACK)]
            for t in range(PACK):
                nc.vector.tensor_tensor(
                    us[t][:], tabs[t][:].indirect(n1_t[:, entries(c)]), ys[t][:, columns(c)], ALU.subtract
                )
            return us

        def weave(c, z):
            woven = sbuf("z_woven%d" % c, [P, N, PACK], BF16)
            nc.vector.tensor_copy(*weaving(woven, z))
            return woven

        def quantise(c, woven):
            z_w = sbuf("z_w%d" % c, [P, N], U32)
            z_s = sbuf("z_s%d" % c, [P, N], U8)
            nc.vector.quantize_mx(out=z_w[:].bitcast(FP8X4), scales=z_s[:], in_=woven[:].rearrange("p c t -> p (c t)"))
            return z_w, z_s

        def product(out, t, z_w, z_s):
            nc.tensor.matmul_mx(
                out=out,
                lhsT=d_w[:, P * t : P * (t + 1)].bitcast(FP8X4),
                lhsT_scale=d_plane[:, P * t : P * (t + 1)],
                rhs=z_w[:].bitcast(FP8X4),
                rhs_scale=z_s[:],
                start=True,
                stop=True,
            )

        def inverse_roots(name, root, h_ps):
            h_size = sbuf("h_size" + name, list(root.shape), F32)
            nc.scalar.activation(h_size[:], h_ps, ACT.Abs, scale=0.0625)
            nc.scalar.activation(root, h_size[:], ACT.Abs_reciprocal_sqrt, bias=0.5)

        last = STRIPS - 1
        late_roots = sbuf("late_roots", [P, PACK, 2 * N], F32)

        h_banks = []
        z_prev = None
        for c in range(STRIPS):
            us = table_less_y(c)
            if c == 0:
                nc.vector.tensor_copy(
                    d_w[:].bitcast(I32).rearrange("p (t m i) -> p m t i", t=PACK, i=4),
                    dq_w[:].bitcast(I32).rearrange("p (m i t) -> p m t i", t=PACK, i=4),
                )
            if c > 0:
                woven = weave(c - 1, z_prev)
            g = sbuf("g%d" % c, [P, PACK, N], F32, tag="size%d" % (c - 1))
            size = sbuf("size%d" % c, [P, PACK, N], F32)
            z = sbuf("z%d" % c, [P, PACK, N], BF16)
            for t in range(PACK):
                nc.vector.tensor_tensor(g[:, t, :], ys[t][:].indirect(n2_t[:, entries(c)]), us[t][:], ALU.add)
                if c > 0 and t == 0:
                    z_w, z_s = quantise(c - 1, woven)
                if c == last:
                    nc.scalar.activation(size[:, t, :], g[:, t, :], ACT.Abs)
                    nc.scalar.activation(z[:, t, :], size[:, t, :], ACT.Copy, scale=gs_t[:, t : t + 1])
                elif t % 2 == 1:
                    nc.scalar.activation(size[:, t - 1 : t + 1, :], g[:, t - 1 : t + 1, :], ACT.Abs)
                    for r in (t - 1, t):
                        nc.scalar.activation(z[:, r, :], size[:, r, :], ACT.Copy, scale=gs_t[:, r : r + 1])
            if c > 0:
                h_ps = ps.tile([P, PACK, N], F32, name="h_ps%d" % (c - 1))
                for t in range(PACK):
                    product(h_ps[:, t, :], t, z_w, z_s)
                if c == last:
                    inverse_roots("%d" % (c - 1), late_roots[:, :, 0:N], h_ps[:])
                else:
                    root = sbuf("root%d" % (c - 1), [P, PACK, N], F32)
                    inverse_roots("%d" % (c - 1), root[:], h_ps[:])
                    for t in range(PACK):
                        nc.scalar.activation(recips[t][:, columns(c - 1)], root[:, t, :], ACT.Square)
                h_banks.append(h_ps)
            z_prev = z

        woven = weave(last, z_prev)
        z_w, z_s = quantise(last, woven)
        h_last = []
        for t in range(PACK):
            h_ps = ps.tile([P, N], F32, name="h_last%d" % t, tag="plane%d" % t)
            product(h_ps[:], t, z_w, z_s)
            inverse_roots("_last%d" % t, late_roots[:, t, N : 2 * N], h_ps[:])
            nc.scalar.activation(recips[t][:, 2 * N : 4 * N], late_roots[:, t, :], ACT.Square)
            h_last.append(h_ps)
        h_early = sbuf("h_early", [P, PACK, 2 * N], F32, tag="z_woven%d" % last)
        for c in range(2):
            nc.vector.tensor_scalar(h_early[:, :, columns(c)], h_banks[c][:], 0.0625, None, ALU.mult)
        h_late = sbuf("h_late", [P, PACK, 2 * N], F32, tag="late_roots")
        nc.scalar.activation(h_late[:, :, 0:N], h_banks[2][:], ACT.Copy, scale=0.0625)
        for t in range(PACK):
            nc.scalar.activation(h_late[:, t, N : 2 * N], h_last[t][:], ACT.Copy, scale=0.0625)

        out_rows = out_0.rearrange("(p t) c -> p t c", t=PACK)
        out_s = sbuf("out_s", [P, S], U8)
        word_rows = out_1[0].rearrange("p n t -> p (n t)").bitcast(I32)
        for c0, n in OUT_CHUNKS:
            cols = slice(c0, c0 + n)
            h = h_early if c0 < 2 * N else h_late
            h_cols = slice(c0 % (2 * N), c0 % (2 * N) + n)
            res = sbuf("res%d" % c0, [P, PACK, n], F32)
            for t in range(PACK):
                nc.vector.tensor_tensor(
                    res[:, t, :], recips[t][:].indirect(n3_t[:, c0 // 16 : (c0 + n) // 16]), h[:, t, h_cols], ALU.mult
                )
            nc.sync.dma_start(out_rows[:, :, cols], res[:])
            woven = sbuf("res_woven%d" % c0, [P, n, PACK], BF16)
            if c0 + n < S:
                nc.scalar.copy(*weaving(woven, res))
            else:
                nc.vector.tensor_copy(*weaving(woven, res))
            out_w = sbuf("out_w%d" % c0, [P, n], U32)
            nc.vector.quantize_mx(
                out=out_w[:].bitcast(FP8X4), scales=out_s[:, cols], in_=woven[:].rearrange("p c t -> p (c t)")
            )
            nc.sync.dma_start(word_rows[:, cols], out_w[:].bitcast(I32))
        for a in range(PACK):
            queue = nc.sync if a % 2 == 0 else nc.scalar
            queue.dma_start(out_2[0, a:16:4, :].bitcast(I32), out_s[a:P:32, :].bitcast(I32))
